import numpy as np
import ml_dtypes


def mxq(x, axis, fmt="e4m3"):
    dtype, down = {"e4m3": (ml_dtypes.float8_e4m3fn, 7), "e5m2": (ml_dtypes.float8_e5m2, 14)}[fmt]
    v = np.moveaxis(np.asarray(x, np.float32).astype(ml_dtypes.bfloat16).astype(np.float64), axis, -1)
    blocks = v.reshape(v.shape[:-1] + (-1, 32))
    amax = np.abs(blocks).max(-1, keepdims=True)
    byte = np.maximum(np.where(amax > 0, np.frexp(amax)[1] - 1 + 127, 0) - down, 1)
    scale = np.exp2(byte - 127.0)
    codes = (blocks / scale).astype(np.float32).astype(dtype).astype(np.float64)
    return np.moveaxis((codes * scale).reshape(v.shape), -1, axis)


WIDE = False


def mx_kscale(k):
    if not WIDE:
        return np.ones(k)
    levels = np.array([10, -10, 5, -5, 0])
    if k % 512:
        return np.exp2(np.random.permutation(np.resize(levels, k // 32))).repeat(32)
    a = np.empty((k // 512, 16))
    for p in range(k // 512):
        a[p, :8] = np.random.permutation(np.resize(levels, 8))
        for g in range(8):
            far = levels[np.abs(levels - a[p, g]) >= 10]
            a[p, g + 8] = far[np.random.randint(len(far))]
    return np.exp2(a.ravel()).repeat(32)


def f64(x):
    return np.asarray(x).astype(np.float64)


def striped(idx):
    return np.tile(np.asarray(idx).reshape(-1, 16).T, (8, 1)).astype(np.uint16)


def unstriped(offs):
    return offs[:16].T.reshape(-1).astype(np.int64)


def striped8(idx):
    return np.asarray(idx).reshape(8, -1, 16).transpose(0, 2, 1).reshape(128, -1).astype(np.uint16)


def unstriped8(offs):
    return offs.reshape(8, 16, -1).transpose(0, 2, 1).reshape(8, -1).astype(np.int64)


def pick8(x, idx, run):
    r = np.arange(len(x))
    return x[r[:, None], idx[r % (8 * run) // run]]


E2M1 = np.array([0.0, 0.5, 1.0, 1.5, 2.0, 3.0, 4.0, 6.0, -0.0, -0.5, -1.0, -1.5, -2.0, -3.0, -4.0, -6.0])


def pack_weight(w, fmt):
    k, n = w.shape
    w = f64(np.asarray(w, np.float32).astype(ml_dtypes.bfloat16)).reshape(k // 32, 32, n)
    amax = np.abs(w).max(1)
    if fmt == "e4m3":
        byte = np.frexp(amax)[1] - 1 + 127 - 7
    else:
        mant, ex = np.frexp(amax / 6.0)
        byte = np.where(mant > 0.5, ex, ex - 1) + 127
    byte = np.clip(np.where(amax > 0, byte, 1), 1, 254)
    scaled = (w * np.exp2(127.0 - byte)[:, None, :]).reshape(k, n).astype(np.float32)
    by_word = np.ascontiguousarray(scaled.reshape(k // 512, 128, 4, n).transpose(0, 1, 3, 2))
    if fmt == "e4m3":
        words = by_word.astype(ml_dtypes.float8_e4m3fn).view(np.uint8)
    else:
        c = by_word.astype(ml_dtypes.float4_e2m1fn).view(np.uint8) & 0xF
        words = (c[..., 0::2] | (c[..., 1::2] << 4)).reshape(k // 512, 128, 2 * n)
    return np.ascontiguousarray(words), np.ascontiguousarray(byte.astype(np.uint8).reshape(k // 512, 16, n))


def unpack_weight(words, scales, fmt):
    g, _, n = scales.shape
    words = np.ascontiguousarray(words).reshape(g, 128, n, -1)
    if fmt == "e4m3":
        vals = words.view(ml_dtypes.float8_e4m3fn).astype(np.float64)
    else:
        nib = np.empty((g, 128, n, 4), np.uint8)
        nib[..., 0::2] = words & 0xF
        nib[..., 1::2] = words >> 4
        vals = E2M1[nib]
    vals = vals * np.repeat(np.exp2(scales.astype(np.float64) - 127.0), 8, axis=1)[..., None]
    return vals.transpose(0, 1, 3, 2).reshape(g * 512, n)


K, J, R, T, Z, M, C, O, N, S, U = 512, 512, 512, 2048, 512, 1024, 1024, 512, 256, 1024, 1024


def setup_inputs():
    n = np.random.standard_normal
    idx = np.random.permutation(T)[:J]
    idx2 = np.random.permutation(M)[:J]
    idx3 = np.stack([np.random.permutation(C)[:J] for _ in range(8)])
    idx4 = np.stack([np.random.permutation(C)[:J] for _ in range(8)])
    idx5 = np.random.permutation(S)[:N]
    idx6 = np.stack([np.random.permutation(U)[:O] for _ in range(8)])
    idx7 = np.stack([np.random.permutation(U)[:O] for _ in range(8)])
    fk = mx_kscale(K)
    fr = mx_kscale(R)
    fz = mx_kscale(Z)
    xtp = pack_weight(n((K, T)) * fk[:, None], "e4m3")
    wp = pack_weight(n((K, R)) * 1 / np.sqrt(K) / fk[:, None] * fr, "e2m1")
    xop = pack_weight(n((Z, M)) / fz[:, None], "e2m1")
    w2p = pack_weight(n((Z, R)) * 1 / np.sqrt(Z) * fz[:, None] * fr, "e4m3")
    vsp = pack_weight(n((R, S)) * 1 / np.sqrt(R) / fr[:, None], "e4m3")
    return {
        "xt_words": xtp[0],
        "xt_scales": xtp[1],
        "w_words": wp[0],
        "w_scales": wp[1],
        "xo_words": xop[0],
        "xo_scales": xop[1],
        "w2_words": w2p[0],
        "w2_scales": w2p[1],
        "vs_words": vsp[0],
        "vs_scales": vsp[1],
        "offs": striped(idx),
        "offs2": striped(idx2),
        "offs3": striped8(idx3),
        "offs4": striped8(idx4),
        "offs5": striped(idx5),
        "offs6": striped8(idx6),
        "offs7": striped8(idx7),
    }


def reference(xt_words, xt_scales, w_words, w_scales, xo_words, xo_scales, w2_words, w2_scales, vs_words, vs_scales, offs, offs2, offs3, offs4, offs5, offs6, offs7):
    idx = unstriped(offs)
    idx2 = unstriped(offs2)
    idx3 = unstriped8(offs3)
    idx4 = unstriped8(offs4)
    idx5 = unstriped(offs5)
    idx6 = unstriped8(offs6)
    idx7 = unstriped8(offs7)
    xtu = unpack_weight(xt_words, xt_scales, "e4m3")
    wu = unpack_weight(w_words, w_scales, "e2m1")
    xou = unpack_weight(xo_words, xo_scales, "e2m1")
    w2u = unpack_weight(w2_words, w2_scales, "e4m3")
    vsu = unpack_weight(vs_words, vs_scales, "e4m3")
    xtidxg = xtu[:, idx]
    a = wu.T @ xtidxg
    xoidx2g = xou[:, idx2]
    b = w2u.T @ xoidx2g
    pw = np.zeros((R, C))
    pw[np.arange(R)[:, None], idx3[np.arange(R) % 512 // 64]] = a
    pv = np.zeros((R, C))
    pv[np.arange(R)[:, None], idx4[np.arange(R) % 512 // 64]] = b
    pg = pw + pv
    hid = pg.reshape(R, O, C // O).max(axis=2)
    vsidx5g = vsu[:, idx5]
    hidq = mxq(hid, 0, "e4m3")
    p = vsidx5g.T @ hidq
    m0 = np.zeros((N, U))
    m0[np.arange(N)[:, None], idx6[np.arange(N) % 128 // 16]] = p
    m1 = np.zeros((N, U))
    m1[np.arange(N)[:, None], idx7[np.arange(N) % 128 // 16]] = p
    y = m0 - m1
    return y

@@ -1,0 +1,217 @@
+from contextlib import ExitStack
+
+import concourse.mybir as mybir
+
+F32 = mybir.dt.float32
+BF16 = mybir.dt.bfloat16
+I32 = mybir.dt.int32
+U32 = mybir.dt.uint32
+U16 = mybir.dt.uint16
+U8 = mybir.dt.uint8
+FP8X4 = mybir.dt.float8_e4m3fn_x4
+FP4X4 = mybir.dt.float4_e2m1fn_x4
+ALU = mybir.AluOpType
+COPY = mybir.ActivationFunctionType.Copy
+
+P = 128
+J, R, T, M, C, O, N, S, U = 512, 512, 2048, 1024, 1024, 512, 256, 1024, 1024
+FLOPS = 671088640
+
+
+def tile_picked_tokens_plain_two_pooledboard_store_divergence_kernel(tc, xt_words, xt_scales, w_words, w_scales, xo_words, xo_scales, w2_words, w2_scales,
+        vs_words, vs_scales, offs, offs2, offs3, offs4, offs5, offs6, offs7, out):
+    nc = tc.nc
+    with ExitStack() as ctx:
+        keep = ctx.enter_context(tc.tile_pool(name="keep", bufs=1))
+        psum = ctx.enter_context(tc.psum_pool(name="psum", bufs=8))
+
+        def sb(name, cols, dtype, rows=P, tag=None):
+            shape = [rows] + (list(cols) if isinstance(cols, tuple) else [cols])
+            return keep.tile(shape, dtype, name=name, tag=tag or name, align_bytes=64)
+
+        def load_list(name, src):
+            t = keep.tile(list(src.shape), U16, name=name)
+            nc.sync.dma_start(t[:], src)
+            return t
+
+        def load_words(name, src, cols, dtype, after=None):
+            t = sb(name, cols, dtype, tag=after)
+            nc.sync.dma_start(t[:].bitcast(I32), src.bitcast(I32))
+            return t
+
+        def stage_scales(name, src, cols):
+            t = sb(name, (4, cols // 4), I32, rows=4)
+            nc.sync.dma_start(t[:], src[0].rearrange("(q j) c -> j q c", j=4).bitcast(I32))
+            return t
+
+        def zeroed(name, cols, dtype, after=None):
+            t = sb(name, cols, dtype, tag=after)
+            engine = nc.gpsimd if after else nc.vector
+            if dtype == U8:
+                engine.memset(t[:].bitcast(I32), 0)
+            else:
+                engine.memset(t[:], 0.0)
+            return t
+
+        def spread(plane, staged):
+            for q in range(4):
+                nc.vector.tensor_copy(plane[32 * q : 32 * q + 4, :].bitcast(I32), staged[:, q, :])
+
+        def load_plane(name, src, cols, after):
+            t = zeroed(name, cols, U8, after)
+            for q in range(4):
+                nc.sync.dma_start(t[32 * q : 32 * q + 4, :].bitcast(I32), src[0, 4 * q : 4 * q + 4, :].bitcast(I32))
+            return t
+
+        def entries(lst, lo, hi):
+            return lst[:, lo // 16 : hi // 16]
+
+        def gather(name, window, lst, lo, hi, dtype):
+            t = sb(name, hi - lo, dtype)
+            nc.vector.tensor_copy(t[:], window[:].indirect(entries(lst, lo, hi)))
+            return t
+
+        def scatter(board, lst, lo, hi, src):
+            nc.scalar.activation(board[:].indirect(entries(lst, lo, hi)), src, COPY)
+
+        w2s_st = stage_scales("w2s_st", w2_scales, R)
+        w2_raw = load_words("w2_raw", w2_words[0].rearrange("p n t -> p (n t)"), R, U32)
+        xos_plane = load_plane("xos_plane", xo_scales, M, None)
+        l2 = load_list("l2", offs2)
+        xo_w = load_words("xo_w", xo_words[0], M, U16)
+        l4 = load_list("l4", offs4)
+
+        w2s_plane = zeroed("w2s_plane", R, U8)
+        pv = [zeroed("pv0", C, F32), zeroed("pv1", C, F32)]
+        spread(w2s_plane, w2s_st)
+        w2s = sb("w2s", R, U8)
+        nc.vector.tensor_copy(w2s[:].rearrange("p (t m) -> p t m", t=4), w2s_plane[:].rearrange("p (m t) -> p t m", t=4))
+        w2 = sb("w2", R, U32)
+        nc.scalar.copy(w2[:].rearrange("p (t m) -> p m t", t=4), w2_raw[:].rearrange("p (m t) -> p m t", t=4))
+
+        b_cuts = [(0, 128), (128, 256), (256, 512)]
+        xo_g = []
+
+        def b_product(acc, t, piece):
+            words, scales = xo_g[piece]
+            cols = slice(P * t, P * (t + 1))
+            nc.tensor.matmul_mx(acc, lhsT=w2[:, cols].bitcast(FP8X4), lhsT_scale=w2s[:, cols],
+                                rhs=words[:].bitcast(FP4X4), rhs_scale=scales[:], start=True, stop=True)
+
+        for piece, (lo, hi) in enumerate(b_cuts):
+            picked_scales = gather("xo_gs%d" % piece, xos_plane, l2, lo, hi, U8)
+            xo_g.append((gather("xo_gw%d" % piece, xo_w, l2, lo, hi, U16), picked_scales))
+            if piece == 0:
+                acc = psum.tile([P, 512], F32, name="acc")
+                for t in range(2):
+                    b_product(acc[:, P * t : P * (t + 1)], t, piece)
+                b_sb = sb("b_first", 2 * P, F32)
+                nc.scalar.copy(b_sb[:], acc[:, : 2 * P])
+                for t in range(2):
+                    scatter(pv[t], l4, lo, hi, b_sb[:, P * t : P * (t + 1)])
+            else:
+                for t in range(2):
+                    acc = psum.tile([P, 512], F32, name="acc")
+                    b_product(acc[:, : hi - lo], t, piece)
+                    b_sb = sb("b%d_%d" % (t, piece), hi - lo, F32)
+                    nc.vector.tensor_copy(b_sb[:], acc[:, : hi - lo])
+                    scatter(pv[t], l4, lo, hi, b_sb[:])
+        pv.append(zeroed("pv2", C, F32, "b_first"))
+
+        l1 = load_list("l1", offs)
+        xt_w = load_words("xt_w", xt_words[0].rearrange("p n t -> p (n t)"), T, U32, "w2s_st")
+        w_raw = load_words("w_raw", w_words[0], 2 * R, U8, "w2s_plane")
+        xts_plane = load_plane("xts_plane", xt_scales, T, "b0_1")
+        ws_plane = load_plane("ws_plane", w_scales, R, "b1_1")
+        l3 = load_list("l3", offs3)
+        l5 = load_list("l5", offs5)
+        vs_w = load_words("vs_w", vs_words[0].rearrange("p n t -> p (n t)"), S, U32, "w2_raw")
+        vss_plane = load_plane("vss_plane", vs_scales, S, "xos_plane")
+        l6 = load_list("l6", offs6)
+        l7 = load_list("l7", offs7)
+
+        pv.append(zeroed("pv3", C, F32, "b0_2"))
+        for t in range(2, 4):
+            acc = psum.tile([P, 512], F32, name="acc")
+            for piece, (lo, hi) in enumerate(b_cuts):
+                b_product(acc[:, lo:hi], t, piece)
+            b_sb = sb("b%d" % t, J, F32)
+            nc.vector.tensor_copy(b_sb[:], acc[:])
+            scatter(pv[t], l4, 0, J, b_sb[:])
+
+        xt_gw = gather("xt_gw", xt_w, l1, 0, J, U32)
+        xt_gs = gather("xt_gs", xts_plane, l1, 0, J, U8)
+        ws = sb("ws", R, U8)
+        nc.vector.tensor_copy(ws[:].rearrange("p (t m) -> p t m", t=4), ws_plane[:].rearrange("p (m t) -> p t m", t=4))
+        w = sb("w", 2 * R, U8)
+        nc.vector.tensor_copy(w[:].rearrange("p (t m e) -> p t m e", t=4, e=2), w_raw[:].rearrange("p (m t e) -> p t m e", t=4, e=2))
+        pw = [zeroed("pw0", C, F32, "b1_2"), zeroed("pw1", C, F32, "b2")]
+        a_sb = []
+        for t in range(4):
+            acc = psum.tile([P, 512], F32, name="acc")
+            nc.tensor.matmul_mx(acc[:], lhsT=w[:, 2 * P * t : 2 * P * (t + 1)].bitcast(FP4X4), lhsT_scale=ws[:, P * t : P * (t + 1)],
+                                rhs=xt_gw[:].bitcast(FP8X4), rhs_scale=xt_gs[:], start=True, stop=True)
+            a_sb.append(sb("a%d" % t, J, F32))
+            nc.vector.tensor_copy(a_sb[t][:], acc[:])
+
+        vs_gw = gather("vs_gw", vs_w, l5, 0, N, U32)
+        vs_gs = gather("vs_gs", vss_plane, l5, 0, N, U8)
+
+        o_cuts = [(0, 128), (128, 512)]
+        hid = [sb("hid%d" % i, (hi - lo, 4), BF16) for i, (lo, hi) in enumerate(o_cuts)]
+
+        def pool_piece(t, i):
+            lo, hi = o_cuts[i]
+            pg = sb("pg%d_%d" % (t, i), 2 * (hi - lo), F32, tag="hid0" if (t, i) == (3, 1) else None)
+            nc.vector.tensor_tensor(pg[:], pw[t % 2][:, 2 * lo : 2 * hi], pv[t][:, 2 * lo : 2 * hi], ALU.add)
+            pairs = pg[:].rearrange("p (o c) -> p o c", c=2)
+            nc.vector.tensor_tensor(hid[i][:, :, t], pairs[:, :, 0], pairs[:, :, 1], ALU.max)
+
+        for t in range(4):
+            scatter(pw[t % 2], l3, 0, J, a_sb[t][:])
+            if t < 3:
+                for i in range(len(o_cuts)):
+                    pool_piece(t, i)
+
+        freed = [["w2s_st", "w2_raw"], ["b3", "a0"]]
+        pages = [[zeroed("m%d_%d" % (k, u), U, F32, freed[u][k]) for k in range(2)] for u in range(2)]
+        lists = [l6, l7]
+        for i, (lo, hi) in enumerate(o_cuts):
+            width = hi - lo
+            pool_piece(3, i)
+            hw = sb("hw%d" % i, width, U32)
+            hs = sb("hs%d" % i, width, U8)
+            nc.vector.quantize_mx(hw[:].bitcast(FP8X4), hs[:], hid[i][:].rearrange("p o t -> p (o t)"))
+
+            def p_product(dst, u, c0, c1):
+                cols = slice(P * u, P * (u + 1))
+                nc.tensor.matmul_mx(dst, lhsT=vs_gw[:, cols].bitcast(FP8X4), lhsT_scale=vs_gs[:, cols],
+                                    rhs=hw[:, c0:c1].bitcast(FP8X4), rhs_scale=hs[:, c0:c1], start=True, stop=True)
+
+            if i == 0:
+                acc = psum.tile([P, 512], F32, name="acc")
+                for u in range(2):
+                    p_product(acc[:, P * u : P * (u + 1)], u, 0, P)
+                p_sb = sb("p_first", 2 * P, F32)
+                nc.scalar.copy(p_sb[:], acc[:, : 2 * P])
+                for u in range(2):
+                    for k in range(2):
+                        scatter(pages[u][k], lists[k], lo, hi, p_sb[:, P * u : P * (u + 1)])
+            else:
+                for u in range(2):
+                    acc = psum.tile([P, 512], F32, name="acc")
+                    for c0, c1 in [(0, 256), (256, 384)]:
+                        p_product(acc[:, c0:c1], u, c0, c1)
+                    p_sb = sb("p%d_%d" % (u, i), width, F32)
+                    nc.vector.tensor_copy(p_sb[:], acc[:, :width])
+                    for k in range(2):
+                        scatter(pages[u][k], lists[k], lo, hi, p_sb[:])
+
+        for u in range(2):
+            parts = 1 if u == 0 else 4
+            step = U // parts
+            for c in range(parts):
+                cols = slice(c * step, (c + 1) * step)
+                res = sb("res%d_%d" % (u, c), step, F32)
+                nc.vector.tensor_tensor(res[:], pages[u][0][:, cols], pages[u][1][:, cols], ALU.subtract)
+                nc.sync.dma_start(out[P * u : P * (u + 1), cols], res[:])

@@ -44,13 +44,9 @@ def tile_picked_tokens_plain_two_pooledboard_store_divergence_kernel(tc, xt_word
             nc.sync.dma_start(t[:], src[0].rearrange("(q j) c -> j q c", j=4).bitcast(I32))
             return t
 
-        def zeroed(name, cols, dtype, after=None):
+        def zeroed(name, cols, dtype, after=None, engine=nc.gpsimd):
             t = sb(name, cols, dtype, tag=after)
-            engine = nc.gpsimd if after else nc.vector
-            if dtype == U8:
-                engine.memset(t[:].bitcast(I32), 0)
-            else:
-                engine.memset(t[:], 0.0)
+            engine.memset(t[:].bitcast(I32), 0)
             return t
 
         def spread(plane, staged):
@@ -75,48 +71,51 @@ def tile_picked_tokens_plain_two_pooledboard_store_divergence_kernel(tc, xt_word
             nc.scalar.activation(board[:].indirect(entries(lst, lo, hi)), src, COPY)
 
         w2s_st = stage_scales("w2s_st", w2_scales, R)
-        w2_raw = load_words("w2_raw", w2_words[0].rearrange("p n t -> p (n t)"), R, U32)
+        xo_w = load_words("xo_w", xo_words[0], M, U16)
         xos_plane = load_plane("xos_plane", xo_scales, M, None)
         l2 = load_list("l2", offs2)
-        xo_w = load_words("xo_w", xo_words[0], M, U16)
+        w2_raw = load_words("w2_raw", w2_words[0].rearrange("p n t -> p (n t)"), R, U32)
         l4 = load_list("l4", offs4)
 
         w2s_plane = zeroed("w2s_plane", R, U8)
-        pv = [zeroed("pv0", C, F32), zeroed("pv1", C, F32)]
+        pv = [zeroed("pv0", C, F32, engine=nc.vector), zeroed("pv1", C, F32)]
         spread(w2s_plane, w2s_st)
-        w2s = sb("w2s", R, U8)
-        nc.vector.tensor_copy(w2s[:].rearrange("p (t m) -> p t m", t=4), w2s_plane[:].rearrange("p (m t) -> p t m", t=4))
-        w2 = sb("w2", R, U32)
-        nc.scalar.copy(w2[:].rearrange("p (t m) -> p m t", t=4), w2_raw[:].rearrange("p (m t) -> p m t", t=4))
+        w2s = [sb("w2s%d" % h, 2 * P, U8) for h in range(2)]
+        w2 = [sb("w2_%d" % h, 2 * P, U32) for h in range(2)]
+
+        def dealt(src, h):
+            return src.rearrange("p (m t) -> p t m", t=4)[:, 2 * h : 2 * h + 2, :]
+
+        nc.vector.tensor_copy(w2s[0][:].rearrange("p (t m) -> p t m", t=2), dealt(w2s_plane[:], 0))
+        nc.scalar.copy(w2[0][:].rearrange("p (t m) -> p m t", t=2), w2_raw[:].rearrange("p (m t) -> p m t", t=4)[:, :, 0:2])
 
         b_cuts = [(0, 128), (128, 256), (256, 512)]
         xo_g = []
 
         def b_product(acc, t, piece):
             words, scales = xo_g[piece]
-            cols = slice(P * t, P * (t + 1))
-            nc.tensor.matmul_mx(acc, lhsT=w2[:, cols].bitcast(FP8X4), lhsT_scale=w2s[:, cols],
+            cols = slice(P * (t % 2), P * (t % 2 + 1))
+            nc.tensor.matmul_mx(acc, lhsT=w2[t // 2][:, cols].bitcast(FP8X4), lhsT_scale=w2s[t // 2][:, cols],
                                 rhs=words[:].bitcast(FP4X4), rhs_scale=scales[:], start=True, stop=True)
 
         for piece, (lo, hi) in enumerate(b_cuts):
             picked_scales = gather("xo_gs%d" % piece, xos_plane, l2, lo, hi, U8)
             xo_g.append((gather("xo_gw%d" % piece, xo_w, l2, lo, hi, U16), picked_scales))
-            if piece == 0:
+            b_sb = []
+            for t in range(2):
                 acc = psum.tile([P, 512], F32, name="acc")
-                for t in range(2):
-                    b_product(acc[:, P * t : P * (t + 1)], t, piece)
-                b_sb = sb("b_first", 2 * P, F32)
-                nc.scalar.copy(b_sb[:], acc[:, : 2 * P])
-                for t in range(2):
-                    scatter(pv[t], l4, lo, hi, b_sb[:, P * t : P * (t + 1)])
-            else:
-                for t in range(2):
-                    acc = psum.tile([P, 512], F32, name="acc")
-                    b_product(acc[:, : hi - lo], t, piece)
-                    b_sb = sb("b%d_%d" % (t, piece), hi - lo, F32)
-                    nc.vector.tensor_copy(b_sb[:], acc[:, : hi - lo])
-                    scatter(pv[t], l4, lo, hi, b_sb[:])
-        pv.append(zeroed("pv2", C, F32, "b_first"))
+                b_product(acc[:, : hi - lo], t, piece)
+                b_sb.append(sb("b%d_%d" % (t, piece), hi - lo, F32))
+                if piece == 0:
+                    nc.scalar.copy(b_sb[t][:], acc[:, : hi - lo])
+                else:
+                    nc.vector.tensor_copy(b_sb[t][:], acc[:, : hi - lo])
+            for t in range(2):
+                scatter(pv[t], l4, lo, hi, b_sb[t][:])
+        nc.vector.tensor_copy(w2s[1][:].rearrange("p (t m) -> p t m", t=2), dealt(w2s_plane[:], 1))
+        nc.vector.tensor_copy(w2[1][:].bitcast(I32).rearrange("p (t m) -> p m t", t=2),
+                              w2_raw[:].bitcast(I32).rearrange("p (m t) -> p m t", t=4)[:, :, 2:4])
+        pv.append(zeroed("pv2", C, F32, "b1_0"))
 
         l1 = load_list("l1", offs)
         xt_w = load_words("xt_w", xt_words[0].rearrange("p n t -> p (n t)"), T, U32, "w2s_st")
@@ -157,61 +156,65 @@ def tile_picked_tokens_plain_two_pooledboard_store_divergence_kernel(tc, xt_word
         vs_gw = gather("vs_gw", vs_w, l5, 0, N, U32)
         vs_gs = gather("vs_gs", vss_plane, l5, 0, N, U8)
 
-        o_cuts = [(0, 128), (128, 512)]
+        o_cuts = [(0, 128), (128, 256), (256, 512)]
         hid = [sb("hid%d" % i, (hi - lo, 4), BF16) for i, (lo, hi) in enumerate(o_cuts)]
 
-        def pool_piece(t, i):
-            lo, hi = o_cuts[i]
-            pg = sb("pg%d_%d" % (t, i), 2 * (hi - lo), F32, tag="hid0" if (t, i) == (3, 1) else None)
+        def add_boards(name, t, lo, hi, after=None):
+            pg = sb(name, 2 * (hi - lo), F32, tag=after)
             nc.vector.tensor_tensor(pg[:], pw[t % 2][:, 2 * lo : 2 * hi], pv[t][:, 2 * lo : 2 * hi], ALU.add)
-            pairs = pg[:].rearrange("p (o c) -> p o c", c=2)
+            return pg[:].rearrange("p (o c) -> p o c", c=2)
+
+        def pool_pairs(t, i, pairs):
             nc.vector.tensor_tensor(hid[i][:, :, t], pairs[:, :, 0], pairs[:, :, 1], ALU.max)
 
         for t in range(4):
             scatter(pw[t % 2], l3, 0, J, a_sb[t][:])
             if t < 3:
-                for i in range(len(o_cuts)):
-                    pool_piece(t, i)
+                pairs = add_boards("pg%d" % t, t, 0, O, "w2_raw")
+                for i, (lo, hi) in enumerate(o_cuts):
+                    pool_pairs(t, i, pairs[:, lo:hi, :])
 
-        freed = [["w2s_st", "w2_raw"], ["b3", "a0"]]
+        freed = [["w2s_st", "b0_1"], ["b3", "a0"]]
         pages = [[zeroed("m%d_%d" % (k, u), U, F32, freed[u][k]) for k in range(2)] for u in range(2)]
         lists = [l6, l7]
+        late = psum.tile([P, 512], F32, name="acc")
         for i, (lo, hi) in enumerate(o_cuts):
             width = hi - lo
-            pool_piece(3, i)
+            pool_pairs(3, i, add_boards("pg3_%d" % i, 3, lo, hi, "hid0" if i else "w2_raw"))
             hw = sb("hw%d" % i, width, U32)
             hs = sb("hs%d" % i, width, U8)
             nc.vector.quantize_mx(hw[:].bitcast(FP8X4), hs[:], hid[i][:].rearrange("p o t -> p (o t)"))
 
-            def p_product(dst, u, c0, c1):
+            def p_product(dst, u):
                 cols = slice(P * u, P * (u + 1))
                 nc.tensor.matmul_mx(dst, lhsT=vs_gw[:, cols].bitcast(FP8X4), lhsT_scale=vs_gs[:, cols],
-                                    rhs=hw[:, c0:c1].bitcast(FP8X4), rhs_scale=hs[:, c0:c1], start=True, stop=True)
+                                    rhs=hw[:].bitcast(FP8X4), rhs_scale=hs[:], start=True, stop=True)
 
-            if i == 0:
+            ready = []
+            for u in range(2):
+                if u == 1 and i > 0:
+                    p_product(late[:, lo - P : hi - P], u)
+                    continue
                 acc = psum.tile([P, 512], F32, name="acc")
-                for u in range(2):
-                    p_product(acc[:, P * u : P * (u + 1)], u, 0, P)
-                p_sb = sb("p_first", 2 * P, F32)
-                nc.scalar.copy(p_sb[:], acc[:, : 2 * P])
-                for u in range(2):
-                    for k in range(2):
-                        scatter(pages[u][k], lists[k], lo, hi, p_sb[:, P * u : P * (u + 1)])
-            else:
-                for u in range(2):
-                    acc = psum.tile([P, 512], F32, name="acc")
-                    for c0, c1 in [(0, 256), (256, 384)]:
-                        p_product(acc[:, c0:c1], u, c0, c1)
-                    p_sb = sb("p%d_%d" % (u, i), width, F32)
+                p_product(acc[:, :width], u)
+                p_sb = sb("p%d_%d" % (u, i), width, F32)
+                if i == 0:
+                    nc.scalar.copy(p_sb[:], acc[:, :width])
+                else:
                     nc.vector.tensor_copy(p_sb[:], acc[:, :width])
-                    for k in range(2):
-                        scatter(pages[u][k], lists[k], lo, hi, p_sb[:])
+                ready.append((u, p_sb))
+            for u, p_sb in ready:
+                for k in range(2):
+                    scatter(pages[u][k], lists[k], lo, hi, p_sb[:])
+        p_late = sb("p_late", O - P, F32)
+        nc.vector.tensor_copy(p_late[:], late[:, : O - P])
+        for k in range(2):
+            scatter(pages[1][k], lists[k], P, O, p_late[:])
 
         for u in range(2):
-            parts = 1 if u == 0 else 4
-            step = U // parts
-            for c in range(parts):
-                cols = slice(c * step, (c + 1) * step)
-                res = sb("res%d_%d" % (u, c), step, F32)
+            cuts = [0, U] if u == 0 else [0, 320, 640, 896, U]
+            for c in range(len(cuts) - 1):
+                cols = slice(cuts[c], cuts[c + 1])
+                res = sb("res%d_%d" % (u, c), cuts[c + 1] - cuts[c], F32)
                 nc.vector.tensor_tensor(res[:], pages[u][0][:, cols], pages[u][1][:, cols], ALU.subtract)
                 nc.sync.dma_start(out[P * u : P * (u + 1), cols], res[:])

@@ -120,23 +120,24 @@ def tile_picked_tokens_plain_two_pooledboard_store_divergence_kernel(tc, xt_word
         l1 = load_list("l1", offs)
         xt_w = load_words("xt_w", xt_words[0].rearrange("p n t -> p (n t)"), T, U32, "w2s_st")
         w_raw = load_words("w_raw", w_words[0], 2 * R, U8, "w2s_plane")
-        xts_plane = load_plane("xts_plane", xt_scales, T, "b0_1")
-        ws_plane = load_plane("ws_plane", w_scales, R, "b1_1")
+        xts_plane = load_plane("xts_plane", xt_scales, T, "b0_0")
+        ws_plane = load_plane("ws_plane", w_scales, R, "xos_plane")
         l3 = load_list("l3", offs3)
         l5 = load_list("l5", offs5)
         vs_w = load_words("vs_w", vs_words[0].rearrange("p n t -> p (n t)"), S, U32, "w2_raw")
-        vss_plane = load_plane("vss_plane", vs_scales, S, "xos_plane")
+        vss_plane = load_plane("vss_plane", vs_scales, S, "b0_1")
         l6 = load_list("l6", offs6)
         l7 = load_list("l7", offs7)
 
-        pv.append(zeroed("pv3", C, F32, "b0_2"))
-        for t in range(2, 4):
+        def b_whole(t):
             acc = psum.tile([P, 512], F32, name="acc")
             for piece, (lo, hi) in enumerate(b_cuts):
                 b_product(acc[:, lo:hi], t, piece)
             b_sb = sb("b%d" % t, J, F32)
             nc.vector.tensor_copy(b_sb[:], acc[:])
-            scatter(pv[t], l4, 0, J, b_sb[:])
+            return b_sb
+
+        scatter(pv[2], l4, 0, J, b_whole(2)[:])
 
         xt_gw = gather("xt_gw", xt_w, l1, 0, J, U32)
         xt_gs = gather("xt_gs", xts_plane, l1, 0, J, U8)
@@ -144,7 +145,7 @@ def tile_picked_tokens_plain_two_pooledboard_store_divergence_kernel(tc, xt_word
         nc.vector.tensor_copy(ws[:].rearrange("p (t m) -> p t m", t=4), ws_plane[:].rearrange("p (m t) -> p t m", t=4))
         w = sb("w", 2 * R, U8)
         nc.vector.tensor_copy(w[:].rearrange("p (t m e) -> p t m e", t=4, e=2), w_raw[:].rearrange("p (m t e) -> p t m e", t=4, e=2))
-        pw = [zeroed("pw0", C, F32, "b1_2"), zeroed("pw1", C, F32, "b2")]
+        pw = [zeroed("pw0", C, F32, "b1_1"), zeroed("pw1", C, F32, "b0_2")]
         a_sb = []
         for t in range(4):
             acc = psum.tile([P, 512], F32, name="acc")
@@ -153,6 +154,7 @@ def tile_picked_tokens_plain_two_pooledboard_store_divergence_kernel(tc, xt_word
             a_sb.append(sb("a%d" % t, J, F32))
             nc.vector.tensor_copy(a_sb[t][:], acc[:])
 
+        b_last = b_whole(3)
         vs_gw = gather("vs_gw", vs_w, l5, 0, N, U32)
         vs_gs = gather("vs_gs", vss_plane, l5, 0, N, U8)
 
@@ -161,20 +163,22 @@ def tile_picked_tokens_plain_two_pooledboard_store_divergence_kernel(tc, xt_word
 
         def add_boards(name, t, lo, hi, after=None):
             pg = sb(name, 2 * (hi - lo), F32, tag=after)
-            nc.vector.tensor_tensor(pg[:], pw[t % 2][:, 2 * lo : 2 * hi], pv[t][:, 2 * lo : 2 * hi], ALU.add)
+            nc.vector.tensor_tensor(pg[:], pw[t % 2][:, 2 * lo : 2 * hi], pv[t % 3][:, 2 * lo : 2 * hi], ALU.add)
             return pg[:].rearrange("p (o c) -> p o c", c=2)
 
         def pool_pairs(t, i, pairs):
             nc.vector.tensor_tensor(hid[i][:, :, t], pairs[:, :, 0], pairs[:, :, 1], ALU.max)
 
         for t in range(4):
+            if t == 3:
+                scatter(pv[0], l4, 0, J, b_last[:])
             scatter(pw[t % 2], l3, 0, J, a_sb[t][:])
             if t < 3:
                 pairs = add_boards("pg%d" % t, t, 0, O, "w2_raw")
                 for i, (lo, hi) in enumerate(o_cuts):
                     pool_pairs(t, i, pairs[:, lo:hi, :])
 
-        freed = [["w2s_st", "b0_1"], ["b3", "a0"]]
+        freed = [["w2s_st", "b0_0"], ["b2", "a0"]]
         pages = [[zeroed("m%d_%d" % (k, u), U, F32, freed[u][k]) for k in range(2)] for u in range(2)]
         lists = [l6, l7]
         late = psum.tile([P, 512], F32, name="acc")

@@ -53,8 +53,8 @@ def tile_picked_tokens_plain_two_pooledboard_store_divergence_kernel(tc, xt_word
             for q in range(4):
                 nc.vector.tensor_copy(plane[32 * q : 32 * q + 4, :].bitcast(I32), staged[:, q, :])
 
-        def load_plane(name, src, cols, after):
-            t = zeroed(name, cols, U8, after)
+        def load_plane(name, src, cols, after, engine=nc.gpsimd):
+            t = zeroed(name, cols, U8, after, engine)
             for q in range(4):
                 nc.sync.dma_start(t[32 * q : 32 * q + 4, :].bitcast(I32), src[0, 4 * q : 4 * q + 4, :].bitcast(I32))
             return t
@@ -72,13 +72,13 @@ def tile_picked_tokens_plain_two_pooledboard_store_divergence_kernel(tc, xt_word
 
         w2s_st = stage_scales("w2s_st", w2_scales, R)
         xo_w = load_words("xo_w", xo_words[0], M, U16)
-        xos_plane = load_plane("xos_plane", xo_scales, M, None)
+        xos_plane = load_plane("xos_plane", xo_scales, M, None, nc.vector)
         l2 = load_list("l2", offs2)
         w2_raw = load_words("w2_raw", w2_words[0].rearrange("p n t -> p (n t)"), R, U32)
         l4 = load_list("l4", offs4)
 
-        w2s_plane = zeroed("w2s_plane", R, U8)
-        pv = [zeroed("pv0", C, F32, engine=nc.vector), zeroed("pv1", C, F32)]
+        w2s_plane = zeroed("w2s_plane", R, U8, engine=nc.vector)
+        pv = [zeroed("pv0", C, F32, engine=nc.vector), zeroed("pv1", C, F32, engine=nc.vector)]
         spread(w2s_plane, w2s_st)
         w2s = [sb("w2s%d" % h, 2 * P, U8) for h in range(2)]
         w2 = [sb("w2_%d" % h, 2 * P, U32) for h in range(2)]

@@ -115,17 +115,16 @@ def tile_picked_tokens_plain_two_pooledboard_store_divergence_kernel(tc, xt_word
         nc.vector.tensor_copy(w2s[1][:].rearrange("p (t m) -> p t m", t=2), dealt(w2s_plane[:], 1))
         nc.vector.tensor_copy(w2[1][:].bitcast(I32).rearrange("p (t m) -> p m t", t=2),
                               w2_raw[:].bitcast(I32).rearrange("p (m t) -> p m t", t=4)[:, :, 2:4])
-        pv.append(zeroed("pv2", C, F32, "b1_0"))
+        pv.append(zeroed("pv2", C, F32, "w2_0", nc.vector))
 
         l1 = load_list("l1", offs)
         xt_w = load_words("xt_w", xt_words[0].rearrange("p n t -> p (n t)"), T, U32, "w2s_st")
         w_raw = load_words("w_raw", w_words[0], 2 * R, U8, "w2s_plane")
-        xts_plane = load_plane("xts_plane", xt_scales, T, "b0_0")
-        ws_plane = load_plane("ws_plane", w_scales, R, "xos_plane")
+        xts_plane = load_plane("xts_plane", xt_scales, T, "xo_w", nc.vector)
+        ws_plane = load_plane("ws_plane", w_scales, R, "xos_plane", nc.vector)
         l3 = load_list("l3", offs3)
         l5 = load_list("l5", offs5)
         vs_w = load_words("vs_w", vs_words[0].rearrange("p n t -> p (n t)"), S, U32, "w2_raw")
-        vss_plane = load_plane("vss_plane", vs_scales, S, "b0_1")
         l6 = load_list("l6", offs6)
         l7 = load_list("l7", offs7)
 
@@ -141,19 +140,22 @@ def tile_picked_tokens_plain_two_pooledboard_store_divergence_kernel(tc, xt_word
 
         xt_gw = gather("xt_gw", xt_w, l1, 0, J, U32)
         xt_gs = gather("xt_gs", xts_plane, l1, 0, J, U8)
-        ws = sb("ws", R, U8)
-        nc.vector.tensor_copy(ws[:].rearrange("p (t m) -> p t m", t=4), ws_plane[:].rearrange("p (m t) -> p t m", t=4))
-        w = sb("w", 2 * R, U8)
-        nc.vector.tensor_copy(w[:].rearrange("p (t m e) -> p t m e", t=4, e=2), w_raw[:].rearrange("p (m t e) -> p t m e", t=4, e=2))
-        pw = [zeroed("pw0", C, F32, "b1_1"), zeroed("pw1", C, F32, "b0_2")]
+        pw = [zeroed("pw0", C, F32, "w2s0", nc.vector), zeroed("pw1", C, F32, "b2")]
         a_sb = []
-        for t in range(4):
-            acc = psum.tile([P, 512], F32, name="acc")
-            nc.tensor.matmul_mx(acc[:], lhsT=w[:, 2 * P * t : 2 * P * (t + 1)].bitcast(FP4X4), lhsT_scale=ws[:, P * t : P * (t + 1)],
-                                rhs=xt_gw[:].bitcast(FP8X4), rhs_scale=xt_gs[:], start=True, stop=True)
-            a_sb.append(sb("a%d" % t, J, F32))
-            nc.vector.tensor_copy(a_sb[t][:], acc[:])
+        for t0, t1 in [(0, 1), (1, 4)]:
+            ws = sb("ws%d" % t0, (t1 - t0) * P, U8)
+            nc.vector.tensor_copy(ws[:].rearrange("p (t m) -> p t m", m=P), ws_plane[:].rearrange("p (m t) -> p t m", t=4)[:, t0:t1, :])
+            w = sb("w%d" % t0, (t1 - t0) * 2 * P, U8)
+            nc.vector.tensor_copy(w[:].rearrange("p (t m e) -> p t m e", m=P, e=2),
+                                  w_raw[:].rearrange("p (m t e) -> p t m e", t=4, e=2)[:, t0:t1, :, :])
+            for t in range(t1 - t0):
+                acc = psum.tile([P, 512], F32, name="acc")
+                nc.tensor.matmul_mx(acc[:], lhsT=w[:, 2 * P * t : 2 * P * (t + 1)].bitcast(FP4X4), lhsT_scale=ws[:, P * t : P * (t + 1)],
+                                    rhs=xt_gw[:].bitcast(FP8X4), rhs_scale=xt_gs[:], start=True, stop=True)
+                a_sb.append(sb("a%d" % (t0 + t), J, F32))
+                nc.vector.tensor_copy(a_sb[t0 + t][:], acc[:])
 
+        vss_plane = load_plane("vss_plane", vs_scales, S, "xos_plane", nc.vector)
         b_last = b_whole(3)
         vs_gw = gather("vs_gw", vs_w, l5, 0, N, U32)
         vs_gs = gather("vs_gs", vss_plane, l5, 0, N, U8)
@@ -178,7 +180,7 @@ def tile_picked_tokens_plain_two_pooledboard_store_divergence_kernel(tc, xt_word
                 for i, (lo, hi) in enumerate(o_cuts):
                     pool_pairs(t, i, pairs[:, lo:hi, :])
 
-        freed = [["w2s_st", "b0_0"], ["b2", "a0"]]
+        freed = [["a0", "a1"], ["a2", "b3"]]
         pages = [[zeroed("m%d_%d" % (k, u), U, F32, freed[u][k]) for k in range(2)] for u in range(2)]
         lists = [l6, l7]
         late = psum.tile([P, 512], F32, name="acc")

from contextlib import ExitStack

import concourse.mybir as mybir

F32 = mybir.dt.float32
BF16 = mybir.dt.bfloat16
I32 = mybir.dt.int32
U32 = mybir.dt.uint32
U16 = mybir.dt.uint16
U8 = mybir.dt.uint8
FP8X4 = mybir.dt.float8_e4m3fn_x4
FP4X4 = mybir.dt.float4_e2m1fn_x4
ALU = mybir.AluOpType
COPY = mybir.ActivationFunctionType.Copy

P = 128
J, R, T, M, C, O, N, S, U = 512, 512, 2048, 1024, 1024, 512, 256, 1024, 1024
FLOPS = 671088640


def tile_picked_tokens_plain_two_pooledboard_store_divergence_kernel(tc, xt_words, xt_scales, w_words, w_scales, xo_words, xo_scales, w2_words, w2_scales,
        vs_words, vs_scales, offs, offs2, offs3, offs4, offs5, offs6, offs7, out):
    nc = tc.nc
    with ExitStack() as ctx:
        keep = ctx.enter_context(tc.tile_pool(name="keep", bufs=1))
        psum = ctx.enter_context(tc.psum_pool(name="psum", bufs=8))

        def sb(name, cols, dtype, rows=P, tag=None):
            shape = [rows] + (list(cols) if isinstance(cols, tuple) else [cols])
            return keep.tile(shape, dtype, name=name, tag=tag or name, align_bytes=64)

        def load_list(name, src):
            t = keep.tile(list(src.shape), U16, name=name)
            nc.sync.dma_start(t[:], src)
            return t

        def load_words(name, src, cols, dtype, after=None):
            t = sb(name, cols, dtype, tag=after)
            nc.sync.dma_start(t[:].bitcast(I32), src.bitcast(I32))
            return t

        def stage_scales(name, src, cols):
            t = sb(name, (4, cols // 4), I32, rows=4)
            nc.sync.dma_start(t[:], src[0].rearrange("(q j) c -> j q c", j=4).bitcast(I32))
            return t

        def zeroed(name, cols, dtype, after=None, engine=nc.gpsimd):
            t = sb(name, cols, dtype, tag=after)
            engine.memset(t[:].bitcast(I32), 0)
            return t

        def spread(plane, staged):
            for q in range(4):
                nc.vector.tensor_copy(plane[32 * q : 32 * q + 4, :].bitcast(I32), staged[:, q, :])

        def load_plane(name, src, cols, after, engine=nc.gpsimd):
            t = zeroed(name, cols, U8, after, engine)
            for q in range(4):
                nc.sync.dma_start(t[32 * q : 32 * q + 4, :].bitcast(I32), src[0, 4 * q : 4 * q + 4, :].bitcast(I32))
            return t

        def entries(lst, lo, hi):
            return lst[:, lo // 16 : hi // 16]

        def gather(name, window, lst, lo, hi, dtype):
            t = sb(name, hi - lo, dtype)
            nc.vector.tensor_copy(t[:], window[:].indirect(entries(lst, lo, hi)))
            return t

        def scatter(board, lst, lo, hi, src):
            nc.scalar.activation(board[:].indirect(entries(lst, lo, hi)), src, COPY)

        w2s_st = stage_scales("w2s_st", w2_scales, R)
        xo_w = load_words("xo_w", xo_words[0], M, U16)
        xos_plane = load_plane("xos_plane", xo_scales, M, None, nc.vector)
        l2 = load_list("l2", offs2)
        w2_raw = load_words("w2_raw", w2_words[0].rearrange("p n t -> p (n t)"), R, U32)
        l4 = load_list("l4", offs4)

        w2s_plane = zeroed("w2s_plane", R, U8, engine=nc.vector)
        pv = [zeroed("pv0", C, F32, engine=nc.vector), zeroed("pv1", C, F32, engine=nc.vector)]
        spread(w2s_plane, w2s_st)
        w2s = [sb("w2s%d" % h, 2 * P, U8) for h in range(2)]
        w2 = [sb("w2_%d" % h, 2 * P, U32) for h in range(2)]

        def dealt(src, h):
            return src.rearrange("p (m t) -> p t m", t=4)[:, 2 * h : 2 * h + 2, :]

        nc.vector.tensor_copy(w2s[0][:].rearrange("p (t m) -> p t m", t=2), dealt(w2s_plane[:], 0))
        nc.scalar.copy(w2[0][:].rearrange("p (t m) -> p m t", t=2), w2_raw[:].rearrange("p (m t) -> p m t", t=4)[:, :, 0:2])

        b_cuts = [(0, 128), (128, 256), (256, 512)]
        xo_g = []

        def b_product(acc, t, piece):
            words, scales = xo_g[piece]
            cols = slice(P * (t % 2), P * (t % 2 + 1))
            nc.tensor.matmul_mx(acc, lhsT=w2[t // 2][:, cols].bitcast(FP8X4), lhsT_scale=w2s[t // 2][:, cols],
                                rhs=words[:].bitcast(FP4X4), rhs_scale=scales[:], start=True, stop=True)

        for piece, (lo, hi) in enumerate(b_cuts):
            picked_scales = gather("xo_gs%d" % piece, xos_plane, l2, lo, hi, U8)
            xo_g.append((gather("xo_gw%d" % piece, xo_w, l2, lo, hi, U16), picked_scales))
            b_sb = []
            for t in range(2):
                acc = psum.tile([P, 512], F32, name="acc")
                b_product(acc[:, : hi - lo], t, piece)
                b_sb.append(sb("b%d_%d" % (t, piece), hi - lo, F32))
                if piece == 0:
                    nc.scalar.copy(b_sb[t][:], acc[:, : hi - lo])
                else:
                    nc.vector.tensor_copy(b_sb[t][:], acc[:, : hi - lo])
            for t in range(2):
                scatter(pv[t], l4, lo, hi, b_sb[t][:])
        nc.vector.tensor_copy(w2s[1][:].rearrange("p (t m) -> p t m", t=2), dealt(w2s_plane[:], 1))
        nc.vector.tensor_copy(w2[1][:].bitcast(I32).rearrange("p (t m) -> p m t", t=2),
                              w2_raw[:].bitcast(I32).rearrange("p (m t) -> p m t", t=4)[:, :, 2:4])
        pv.append(zeroed("pv2", C, F32, "w2_0", nc.vector))

        l1 = load_list("l1", offs)
        xt_w = load_words("xt_w", xt_words[0].rearrange("p n t -> p (n t)"), T, U32, "w2s_st")
        w_raw = load_words("w_raw", w_words[0], 2 * R, U8, "w2s_plane")
        xts_plane = load_plane("xts_plane", xt_scales, T, "xo_w", nc.vector)
        ws_plane = load_plane("ws_plane", w_scales, R, "xos_plane", nc.vector)
        l3 = load_list("l3", offs3)
        l5 = load_list("l5", offs5)
        vs_w = load_words("vs_w", vs_words[0].rearrange("p n t -> p (n t)"), S, U32, "w2_raw")
        l6 = load_list("l6", offs6)
        l7 = load_list("l7", offs7)

        def b_whole(t):
            acc = psum.tile([P, 512], F32, name="acc")
            for piece, (lo, hi) in enumerate(b_cuts):
                b_product(acc[:, lo:hi], t, piece)
            b_sb = sb("b%d" % t, J, F32)
            nc.vector.tensor_copy(b_sb[:], acc[:])
            return b_sb

        scatter(pv[2], l4, 0, J, b_whole(2)[:])

        xt_gw = gather("xt_gw", xt_w, l1, 0, J, U32)
        xt_gs = gather("xt_gs", xts_plane, l1, 0, J, U8)
        pw = [zeroed("pw0", C, F32, "w2s0", nc.vector), zeroed("pw1", C, F32, "b2")]
        a_sb = []
        for t0, t1 in [(0, 1), (1, 4)]:
            ws = sb("ws%d" % t0, (t1 - t0) * P, U8)
            nc.vector.tensor_copy(ws[:].rearrange("p (t m) -> p t m", m=P), ws_plane[:].rearrange("p (m t) -> p t m", t=4)[:, t0:t1, :])
            w = sb("w%d" % t0, (t1 - t0) * 2 * P, U8)
            nc.vector.tensor_copy(w[:].rearrange("p (t m e) -> p t m e", m=P, e=2),
                                  w_raw[:].rearrange("p (m t e) -> p t m e", t=4, e=2)[:, t0:t1, :, :])
            for t in range(t1 - t0):
                acc = psum.tile([P, 512], F32, name="acc")
                nc.tensor.matmul_mx(acc[:], lhsT=w[:, 2 * P * t : 2 * P * (t + 1)].bitcast(FP4X4), lhsT_scale=ws[:, P * t : P * (t + 1)],
                                    rhs=xt_gw[:].bitcast(FP8X4), rhs_scale=xt_gs[:], start=True, stop=True)
                a_sb.append(sb("a%d" % (t0 + t), J, F32))
                nc.vector.tensor_copy(a_sb[t0 + t][:], acc[:])

        vss_plane = load_plane("vss_plane", vs_scales, S, "xos_plane", nc.vector)
        b_last = b_whole(3)
        vs_gw = gather("vs_gw", vs_w, l5, 0, N, U32)
        vs_gs = gather("vs_gs", vss_plane, l5, 0, N, U8)

        o_cuts = [(0, 128), (128, 256), (256, 512)]
        hid = [sb("hid%d" % i, (hi - lo, 4), BF16) for i, (lo, hi) in enumerate(o_cuts)]

        def add_boards(name, t, lo, hi, after=None):
            pg = sb(name, 2 * (hi - lo), F32, tag=after)
            nc.vector.tensor_tensor(pg[:], pw[t % 2][:, 2 * lo : 2 * hi], pv[t % 3][:, 2 * lo : 2 * hi], ALU.add)
            return pg[:].rearrange("p (o c) -> p o c", c=2)

        def pool_pairs(t, i, pairs):
            nc.vector.tensor_tensor(hid[i][:, :, t], pairs[:, :, 0], pairs[:, :, 1], ALU.max)

        for t in range(4):
            if t == 3:
                scatter(pv[0], l4, 0, J, b_last[:])
            scatter(pw[t % 2], l3, 0, J, a_sb[t][:])
            if t < 3:
                pairs = add_boards("pg%d" % t, t, 0, O, "w2_raw")
                for i, (lo, hi) in enumerate(o_cuts):
                    pool_pairs(t, i, pairs[:, lo:hi, :])

        freed = [["a0", "a1"], ["a2", "b3"]]
        pages = [[zeroed("m%d_%d" % (k, u), U, F32, freed[u][k]) for k in range(2)] for u in range(2)]
        lists = [l6, l7]
        late = psum.tile([P, 512], F32, name="acc")
        for i, (lo, hi) in enumerate(o_cuts):
            width = hi - lo
            pool_pairs(3, i, add_boards("pg3_%d" % i, 3, lo, hi, "hid0" if i else "w2_raw"))
            hw = sb("hw%d" % i, width, U32)
            hs = sb("hs%d" % i, width, U8)
            nc.vector.quantize_mx(hw[:].bitcast(FP8X4), hs[:], hid[i][:].rearrange("p o t -> p (o t)"))

            def p_product(dst, u):
                cols = slice(P * u, P * (u + 1))
                nc.tensor.matmul_mx(dst, lhsT=vs_gw[:, cols].bitcast(FP8X4), lhsT_scale=vs_gs[:, cols],
                                    rhs=hw[:].bitcast(FP8X4), rhs_scale=hs[:], start=True, stop=True)

            ready = []
            for u in range(2):
                if u == 1 and i > 0:
                    p_product(late[:, lo - P : hi - P], u)
                    continue
                acc = psum.tile([P, 512], F32, name="acc")
                p_product(acc[:, :width], u)
                p_sb = sb("p%d_%d" % (u, i), width, F32)
                if i == 0:
                    nc.scalar.copy(p_sb[:], acc[:, :width])
                else:
                    nc.vector.tensor_copy(p_sb[:], acc[:, :width])
                ready.append((u, p_sb))
            for u, p_sb in ready:
                for k in range(2):
                    scatter(pages[u][k], lists[k], lo, hi, p_sb[:])
        p_late = sb("p_late", O - P, F32)
        nc.vector.tensor_copy(p_late[:], late[:, : O - P])
        for k in range(2):
            scatter(pages[1][k], lists[k], P, O, p_late[:])

        for u in range(2):
            cuts = [0, U] if u == 0 else [0, 320, 640, 896, U]
            for c in range(len(cuts) - 1):
                cols = slice(cuts[c], cuts[c + 1])
                res = sb("res%d_%d" % (u, c), cuts[c + 1] - cuts[c], F32)
                nc.vector.tensor_tensor(res[:], pages[u][0][:, cols], pages[u][1][:, cols], ALU.subtract)
                nc.sync.dma_start(out[P * u : P * (u + 1), cols], res[:])
